import numpy as np
import ml_dtypes

BF16 = ml_dtypes.bfloat16


def bf(x):
    return np.asarray(x, np.float32).astype(BF16)


def f32(x):
    return np.asarray(x, np.float32)


def f64(x):
    return np.asarray(x).astype(np.float64)


def striped(idx):
    return np.tile(idx.reshape(-1, 16).T, (8, 1))


S, K, H, M, N, E, Q = 512, 256, 128, 128, 256, 2, 128


def setup_inputs():
    return {"base": bf(np.random.standard_normal((M, S))), "x": bf(np.random.standard_normal((K, N))), "w": bf(np.random.standard_normal((E, K, H)) / np.sqrt(K)), "b": f32(0.5 * np.random.standard_normal((H, E))), "w2": bf(1.5 * np.random.standard_normal((E, H, M)) / np.sqrt(H)), "c": f32(0.2 + 0.8 * np.random.random_sample((1, N))), "offs": striped(np.random.permutation(S)[:N])}


def reference(base, x, w, b, w2, c, offs):
    idx = offs[:16].T.reshape(-1)
    z = f64(base).copy()
    for e in range(E):
        t = f64(w)[e].T @ f64(x)[:, e * Q : (e + 1) * Q] + f64(b)[:, e : e + 1]
        t = np.maximum(t, 0.0) * f64(c)[:, e * Q : (e + 1) * Q]
        z[:, idx[e * Q : (e + 1) * Q]] += f64(w2)[e].T @ t
    return z

@@ -1,0 +1,71 @@
+import concourse.mybir as mybir
+from concourse.masks import make_identity
+
+BF16, F32, U16 = mybir.dt.bfloat16, mybir.dt.float32, mybir.dt.uint16
+ADD, MAX, MULT = mybir.AluOpType.add, mybir.AluOpType.max, mybir.AluOpType.mult
+
+P = 128
+S = 512
+K = 256
+N = 256
+E = 2
+Q = N // E
+BLOCKS = K // P
+PER_COLUMN = 16
+
+FLOPS = 2 * N * P * (K + P)
+
+
+def tile_rows_ffnback_relu_kernel(tc, base, x, w, b, w2, c, offs, out):
+    nc = tc.nc
+    with (
+        tc.tile_pool(name="held", bufs=1) as held,
+        tc.psum_pool(name="psum", bufs=1) as psum,
+    ):
+        x_sb = held.tile([P, BLOCKS, N], BF16)
+        nc.sync.dma_start(x_sb[:], x.rearrange("(p a) n -> p a n", a=BLOCKS))
+        w_sb = held.tile([P, E, BLOCKS, P], BF16)
+        nc.sync.dma_start(w_sb[:], w.rearrange("e (p a) h -> p e a h", a=BLOCKS))
+        base_sb = held.tile([P, S], BF16)
+        nc.sync.dma_start(base_sb[:], base)
+        w2_sb = held.tile([P, E, P], BF16)
+        nc.sync.dma_start(w2_sb[:], w2.rearrange("e h m -> h e m"))
+        offsets = held.tile([P, N // PER_COLUMN], U16)
+        nc.sync.dma_start(offsets[:], offs)
+
+        b_sb = held.tile([P, E], F32)
+        nc.scalar.dma_start(b_sb[:], b)
+        c_sb = held.tile([P, N], F32)
+        nc.scalar.dma_start(c_sb[:], c.rearrange("o n -> (o n)").partition_broadcast(P))
+
+        ident = held.tile([P, P], BF16)
+        make_identity(nc, ident[:])
+
+        hidden = [psum.tile([P, Q], F32, name=f"hidden{e}") for e in range(E)]
+        for e in range(E):
+            for a in range(BLOCKS):
+                nc.tensor.matmul(
+                    hidden[e][:],
+                    w_sb[:, e, a, :],
+                    x_sb[:, a, e * Q : (e + 1) * Q],
+                    start=(a == 0),
+                    stop=(a == BLOCKS - 1),
+                )
+
+        window = psum.tile([P, S], F32)
+        nc.tensor.matmul(window[:], ident[:], base_sb[:], start=True, stop=False)
+
+        h_sb = [held.tile([P, Q], BF16, name=f"h{e}") for e in range(E)]
+        for e in range(E):
+            active = held.tile([P, Q], F32, name=f"active{e}")
+            nc.vector.tensor_scalar(active[:], hidden[e][:], b_sb[:, e : e + 1], 0.0, ADD, MAX)
+            nc.vector.tensor_tensor(h_sb[e][:], active[:], c_sb[:, e * Q : (e + 1) * Q], MULT)
+
+        columns = Q // PER_COLUMN
+        for e in range(E):
+            places = window[:].indirect(offsets[:, e * columns : (e + 1) * columns])
+            nc.tensor.matmul(places, w2_sb[:, e, :], h_sb[e][:], start=False, stop=(e == E - 1))
+
+        z_sb = held.tile([P, S], F32)
+        nc.vector.tensor_copy(z_sb[:], window[:])
+        nc.sync.dma_start(out, z_sb[:])

@@ -12,6 +12,7 @@ E = 2
 Q = N // E
 BLOCKS = K // P
 PER_COLUMN = 16
+WARM_UPS = 4
 
 FLOPS = 2 * N * P * (K + P)
 
@@ -33,15 +34,28 @@ def tile_rows_ffnback_relu_kernel(tc, base, x, w, b, w2, c, offs, out):
         offsets = held.tile([P, N // PER_COLUMN], U16)
         nc.sync.dma_start(offsets[:], offs)
 
-        b_sb = held.tile([P, E], F32)
-        nc.scalar.dma_start(b_sb[:], b)
-        c_sb = held.tile([P, N], F32)
-        nc.scalar.dma_start(c_sb[:], c.rearrange("o n -> (o n)").partition_broadcast(P))
+        b_row = held.tile([1, P * E], F32)
+        nc.scalar.dma_start(b_row[:], b.rearrange("(o h) e -> o (h e)", o=1))
+        c_row = held.tile([1, N], F32)
+        nc.scalar.dma_start(c_row[:], c)
+        ones = held.tile([1, P], F32)
+        nc.vector.memset(ones[:], 1.0)
 
         ident = held.tile([P, P], BF16)
         make_identity(nc, ident[:])
 
+        zeros = held.tile([P, S], BF16)
+        nc.vector.memset(zeros[:], 0.0)
+        spare = psum.tile([P, S], F32)
+        for i in range(WARM_UPS):
+            nc.tensor.matmul(spare[:], zeros[:, 0:P], zeros[:], start=True, stop=True)
+
+        b_cols = psum.tile([P, E], F32)
+        for e in range(E):
+            nc.tensor.matmul(b_cols[:, e : e + 1], b_row[:, e::E], ones[:, 0:1], start=True, stop=True)
+
         hidden = [psum.tile([P, Q], F32, name=f"hidden{e}") for e in range(E)]
+        c_all = [psum.tile([P, Q], F32, name=f"c_all{e}") for e in range(E)]
         for e in range(E):
             for a in range(BLOCKS):
                 nc.tensor.matmul(
@@ -51,6 +65,7 @@ def tile_rows_ffnback_relu_kernel(tc, base, x, w, b, w2, c, offs, out):
                     start=(a == 0),
                     stop=(a == BLOCKS - 1),
                 )
+            nc.tensor.matmul(c_all[e][:], ones[:], c_row[:, e * Q : (e + 1) * Q], start=True, stop=True)
 
         window = psum.tile([P, S], F32)
         nc.tensor.matmul(window[:], ident[:], base_sb[:], start=True, stop=False)
@@ -58,8 +73,8 @@ def tile_rows_ffnback_relu_kernel(tc, base, x, w, b, w2, c, offs, out):
         h_sb = [held.tile([P, Q], BF16, name=f"h{e}") for e in range(E)]
         for e in range(E):
             active = held.tile([P, Q], F32, name=f"active{e}")
-            nc.vector.tensor_scalar(active[:], hidden[e][:], b_sb[:, e : e + 1], 0.0, ADD, MAX)
-            nc.vector.tensor_tensor(h_sb[e][:], active[:], c_sb[:, e * Q : (e + 1) * Q], MULT)
+            nc.vector.tensor_scalar(active[:], hidden[e][:], b_cols[:, e : e + 1], 0.0, ADD, MAX)
+            nc.vector.tensor_tensor(h_sb[e][:], active[:], c_all[e][:], MULT)
 
         columns = Q // PER_COLUMN
         for e in range(E):

@@ -27,6 +27,10 @@ def tile_rows_ffnback_relu_kernel(tc, base, x, w, b, w2, c, offs, out):
         nc.sync.dma_start(x_sb[:], x.rearrange("(p a) n -> p a n", a=BLOCKS))
         w_sb = held.tile([P, E, BLOCKS, P], BF16)
         nc.sync.dma_start(w_sb[:], w.rearrange("e (p a) h -> p e a h", a=BLOCKS))
+        b_row = held.tile([1, P * E], F32)
+        nc.sync.dma_start(b_row[:], b.rearrange("(o h) e -> o (h e)", o=1))
+        c_row = held.tile([1, N], F32)
+        nc.sync.dma_start(c_row[:], c)
         base_sb = held.tile([P, S], BF16)
         nc.sync.dma_start(base_sb[:], base)
         w2_sb = held.tile([P, E, P], BF16)
@@ -34,26 +38,18 @@ def tile_rows_ffnback_relu_kernel(tc, base, x, w, b, w2, c, offs, out):
         offsets = held.tile([P, N // PER_COLUMN], U16)
         nc.sync.dma_start(offsets[:], offs)
 
-        b_row = held.tile([1, P * E], F32)
-        nc.scalar.dma_start(b_row[:], b.rearrange("(o h) e -> o (h e)", o=1))
-        c_row = held.tile([1, N], F32)
-        nc.scalar.dma_start(c_row[:], c)
-        ones = held.tile([1, P], F32)
-        nc.vector.memset(ones[:], 1.0)
-
         ident = held.tile([P, P], BF16)
         make_identity(nc, ident[:])
 
         zeros = held.tile([P, S], BF16)
         nc.vector.memset(zeros[:], 0.0)
+        ones = held.tile([1, P], F32)
+        nc.vector.memset(ones[:], 1.0)
         spare = psum.tile([P, S], F32)
         for i in range(WARM_UPS):
             nc.tensor.matmul(spare[:], zeros[:, 0:P], zeros[:], start=True, stop=True)
 
-        b_cols = psum.tile([P, E], F32)
-        for e in range(E):
-            nc.tensor.matmul(b_cols[:, e : e + 1], b_row[:, e::E], ones[:, 0:1], start=True, stop=True)
-
+        b_col = [psum.tile([P, 1], F32, name=f"b_col{e}") for e in range(E)]
         hidden = [psum.tile([P, Q], F32, name=f"hidden{e}") for e in range(E)]
         c_all = [psum.tile([P, Q], F32, name=f"c_all{e}") for e in range(E)]
         for e in range(E):
@@ -65,6 +61,7 @@ def tile_rows_ffnback_relu_kernel(tc, base, x, w, b, w2, c, offs, out):
                     start=(a == 0),
                     stop=(a == BLOCKS - 1),
                 )
+            nc.tensor.matmul(b_col[e][:], b_row[:, e::E], ones[:, 0:1], start=True, stop=True)
             nc.tensor.matmul(c_all[e][:], ones[:], c_row[:, e * Q : (e + 1) * Q], start=True, stop=True)
 
         window = psum.tile([P, S], F32)
@@ -73,7 +70,7 @@ def tile_rows_ffnback_relu_kernel(tc, base, x, w, b, w2, c, offs, out):
         h_sb = [held.tile([P, Q], BF16, name=f"h{e}") for e in range(E)]
         for e in range(E):
             active = held.tile([P, Q], F32, name=f"active{e}")
-            nc.vector.tensor_scalar(active[:], hidden[e][:], b_cols[:, e : e + 1], 0.0, ADD, MAX)
+            nc.vector.tensor_scalar(active[:], hidden[e][:], b_col[e][:], 0.0, ADD, MAX)
             nc.vector.tensor_tensor(h_sb[e][:], active[:], c_all[e][:], MULT)
 
         columns = Q // PER_COLUMN

@@ -12,7 +12,7 @@ E = 2
 Q = N // E
 BLOCKS = K // P
 PER_COLUMN = 16
-WARM_UPS = 4
+WARM_UPS, WARM_UP_COLUMNS = 6, 256
 
 FLOPS = 2 * N * P * (K + P)
 
@@ -41,11 +41,11 @@ def tile_rows_ffnback_relu_kernel(tc, base, x, w, b, w2, c, offs, out):
         ident = held.tile([P, P], BF16)
         make_identity(nc, ident[:])
 
-        zeros = held.tile([P, S], BF16)
+        zeros = held.tile([P, WARM_UP_COLUMNS], BF16)
         nc.vector.memset(zeros[:], 0.0)
         ones = held.tile([1, P], F32)
         nc.vector.memset(ones[:], 1.0)
-        spare = psum.tile([P, S], F32)
+        spare = psum.tile([P, WARM_UP_COLUMNS], F32)
         for i in range(WARM_UPS):
             nc.tensor.matmul(spare[:], zeros[:, 0:P], zeros[:], start=True, stop=True)
 

import concourse.mybir as mybir
from concourse.masks import make_identity

BF16, F32, U16 = mybir.dt.bfloat16, mybir.dt.float32, mybir.dt.uint16
ADD, MAX, MULT = mybir.AluOpType.add, mybir.AluOpType.max, mybir.AluOpType.mult

P = 128
S = 512
K = 256
N = 256
E = 2
Q = N // E
BLOCKS = K // P
PER_COLUMN = 16
WARM_UPS, WARM_UP_COLUMNS = 6, 256

FLOPS = 2 * N * P * (K + P)


def tile_rows_ffnback_relu_kernel(tc, base, x, w, b, w2, c, offs, out):
    nc = tc.nc
    with (
        tc.tile_pool(name="held", bufs=1) as held,
        tc.psum_pool(name="psum", bufs=1) as psum,
    ):
        x_sb = held.tile([P, BLOCKS, N], BF16)
        nc.sync.dma_start(x_sb[:], x.rearrange("(p a) n -> p a n", a=BLOCKS))
        w_sb = held.tile([P, E, BLOCKS, P], BF16)
        nc.sync.dma_start(w_sb[:], w.rearrange("e (p a) h -> p e a h", a=BLOCKS))
        b_row = held.tile([1, P * E], F32)
        nc.sync.dma_start(b_row[:], b.rearrange("(o h) e -> o (h e)", o=1))
        c_row = held.tile([1, N], F32)
        nc.sync.dma_start(c_row[:], c)
        base_sb = held.tile([P, S], BF16)
        nc.sync.dma_start(base_sb[:], base)
        w2_sb = held.tile([P, E, P], BF16)
        nc.sync.dma_start(w2_sb[:], w2.rearrange("e h m -> h e m"))
        offsets = held.tile([P, N // PER_COLUMN], U16)
        nc.sync.dma_start(offsets[:], offs)

        ident = held.tile([P, P], BF16)
        make_identity(nc, ident[:])

        zeros = held.tile([P, WARM_UP_COLUMNS], BF16)
        nc.vector.memset(zeros[:], 0.0)
        ones = held.tile([1, P], F32)
        nc.vector.memset(ones[:], 1.0)
        spare = psum.tile([P, WARM_UP_COLUMNS], F32)
        for i in range(WARM_UPS):
            nc.tensor.matmul(spare[:], zeros[:, 0:P], zeros[:], start=True, stop=True)

        b_col = [psum.tile([P, 1], F32, name=f"b_col{e}") for e in range(E)]
        hidden = [psum.tile([P, Q], F32, name=f"hidden{e}") for e in range(E)]
        c_all = [psum.tile([P, Q], F32, name=f"c_all{e}") for e in range(E)]
        for e in range(E):
            for a in range(BLOCKS):
                nc.tensor.matmul(
                    hidden[e][:],
                    w_sb[:, e, a, :],
                    x_sb[:, a, e * Q : (e + 1) * Q],
                    start=(a == 0),
                    stop=(a == BLOCKS - 1),
                )
            nc.tensor.matmul(b_col[e][:], b_row[:, e::E], ones[:, 0:1], start=True, stop=True)
            nc.tensor.matmul(c_all[e][:], ones[:], c_row[:, e * Q : (e + 1) * Q], start=True, stop=True)

        window = psum.tile([P, S], F32)
        nc.tensor.matmul(window[:], ident[:], base_sb[:], start=True, stop=False)

        h_sb = [held.tile([P, Q], BF16, name=f"h{e}") for e in range(E)]
        for e in range(E):
            active = held.tile([P, Q], F32, name=f"active{e}")
            nc.vector.tensor_scalar(active[:], hidden[e][:], b_col[e][:], 0.0, ADD, MAX)
            nc.vector.tensor_tensor(h_sb[e][:], active[:], c_all[e][:], MULT)

        columns = Q // PER_COLUMN
        for e in range(E):
            places = window[:].indirect(offsets[:, e * columns : (e + 1) * columns])
            nc.tensor.matmul(places, w2_sb[:, e, :], h_sb[e][:], start=False, stop=(e == E - 1))

        z_sb = held.tile([P, S], F32)
        nc.vector.tensor_copy(z_sb[:], window[:])
        nc.sync.dma_start(out, z_sb[:])
